import numpy as np
import ml_dtypes

BF16 = ml_dtypes.bfloat16


def bf(x):
    return np.asarray(x, np.float32).astype(BF16)


def f32(x):
    return np.asarray(x, np.float32)


def f64(x):
    return np.asarray(x).astype(np.float64)


def striped(idx):
    return np.tile(idx.reshape(-1, 16).T, (8, 1))


def rows(idx, k):
    return np.tile(idx, (k, 1))


def look(tab, idx):
    return np.take_along_axis(f64(tab), rows(idx, len(tab)), axis=1)


K, S, H, D, V, N, M = 256, 2048, 256, 2, 512, 1024, 512


def setup_inputs():
    return {"z": bf(np.random.standard_normal((H, S))), "wt": bf(np.random.standard_normal((H, K)) / np.sqrt(H)), "ctr": f32(1.0 * np.random.standard_normal((K, V))), "w": bf(np.random.standard_normal((K, M)) / np.sqrt(K)), "b": f32(0.5 * np.random.standard_normal((M, 1))), "offs": striped(np.random.permutation(S)[:N])}


def reference(z, wt, ctr, w, b, offs):
    idx = offs[:16].T.reshape(-1)
    tab = f64(wt).T @ f64(z)
    x = sum(np.maximum(look(tab, idx[d * V:(d + 1) * V]) - f64(ctr), 0.0) for d in range(D))
    return np.maximum(f64(w).T @ x + f64(b), 0.0)

@@ -1,0 +1,77 @@
+import concourse.mybir as mybir
+
+BF16, F32, U16 = mybir.dt.bfloat16, mybir.dt.float32, mybir.dt.uint16
+RELU = mybir.ActivationFunctionType.Relu
+ADD, MAX, SUBTRACT = mybir.AluOpType.add, mybir.AluOpType.max, mybir.AluOpType.subtract
+
+P = 128
+H, S, R, D, V, M = 256, 2048, 256, 2, 512, 512
+KB, RB, MB = H // P, R // P, M // P
+CHUNK = 512
+FLOPS = 2 * H * R * S + 2 * R * M * V + 3 * R * D * V
+
+
+def tile_lookup_pjedge_relu_kernel(tc, z, wt, ctr, w, b, offs, out):
+    nc = tc.nc
+    with (
+        tc.tile_pool(name="held", bufs=1) as held,
+        tc.tile_pool(name="work", bufs=2) as work,
+        tc.psum_pool(name="psum", bufs=8) as psum,
+    ):
+        wt_sb = held.tile([P, KB, R], BF16)
+        nc.sync.dma_start(wt_sb[:], wt.rearrange("(k p) r -> p k r", p=P))
+        z_sb = held.tile([P, KB, S], BF16)
+        z_view = z.rearrange("(k p) s -> p k s", p=P)
+        for c in range(S // CHUNK):
+            cols = slice(c * CHUNK, (c + 1) * CHUNK)
+            nc.sync.dma_start(z_sb[:, :, cols], z_view[:, :, cols])
+        offsets = held.tile([P, D * V // 16], U16)
+        nc.sync.dma_start(offsets[:], offs)
+        ctr_sb = held.tile([P, RB, V], F32)
+        nc.sync.dma_start(ctr_sb[:], ctr.rearrange("(r p) j -> p r j", p=P))
+        w_sb = held.tile([P, RB, M], BF16)
+        nc.sync.dma_start(w_sb[:], w.rearrange("(r p) m -> p r m", p=P))
+        b_sb = held.tile([P, MB], F32)
+        nc.sync.dma_start(b_sb[:], b.rearrange("(p q) o -> p (q o)", q=MB))
+
+        tables = []
+        for r in range(RB):
+            table = held.tile([P, S], F32, name=f"table{r}")
+            for c in range(S // CHUNK):
+                cols = slice(c * CHUNK, (c + 1) * CHUNK)
+                bank = psum.tile([P, CHUNK], F32, name="bank")
+                for k in range(KB):
+                    nc.tensor.matmul(bank[:], wt_sb[:, k, r * P:(r + 1) * P], z_sb[:, k, cols],
+                                     start=k == 0, stop=k == KB - 1)
+                if r == 0 and c % 2 == 1:
+                    nc.vector.tensor_copy(table[:, cols], bank[:])
+                else:
+                    nc.scalar.copy(table[:, cols], bank[:])
+            tables.append(table)
+
+        xs = []
+        for r in range(RB):
+            diffs = []
+            for d in range(D):
+                diff = work.tile([P, V], F32, name=f"diff{d}")
+                entries = offsets[:, d * V // 16:(d + 1) * V // 16]
+                nc.vector.tensor_tensor(diff[:], tables[r][:].indirect(entries), ctr_sb[:, r, :], SUBTRACT)
+                diffs.append(diff)
+            first = work.tile([P, V], F32, name="first")
+            nc.scalar.activation(first[:], diffs[0][:], RELU)
+            x = held.tile([P, V], BF16, name=f"x{r}")
+            nc.vector.scalar_tensor_tensor(x[:], diffs[1][:], 0.0, first[:], MAX, ADD)
+            xs.append(x)
+
+        out_sb = held.tile([P, MB, V], F32)
+        out_view = out.rearrange("(p q) j -> p q j", q=MB)
+        sums = [psum.tile([P, V], F32, name="bank") for q in range(MB)]
+        for r in range(RB):
+            for q in range(MB):
+                nc.tensor.matmul(sums[q][:], w_sb[:, r, q::MB], xs[r][:], start=r == 0, stop=r == RB - 1)
+        for q in range(MB):
+            if q % 2 == 0:
+                nc.scalar.activation(out_sb[:, q, :], sums[q][:], RELU, bias=b_sb[:, q:q + 1])
+            else:
+                nc.vector.tensor_scalar(out_sb[:, q, :], sums[q][:], b_sb[:, q:q + 1], 0.0, ADD, MAX)
+            nc.sync.dma_start(out_view[:, q, :], out_sb[:, q, :])

@@ -7,6 +7,8 @@ ADD, MAX, SUBTRACT = mybir.AluOpType.add, mybir.AluOpType.max, mybir.AluOpType.s
 P = 128
 H, S, R, D, V, M = 256, 2048, 256, 2, 512, 512
 KB, RB, MB = H // P, R // P, M // P
+HALF = V // 2
+WARM_UP = 5
 CHUNK = 512
 FLOPS = 2 * H * R * S + 2 * R * M * V + 3 * R * D * V
 
@@ -34,6 +36,12 @@ def tile_lookup_pjedge_relu_kernel(tc, z, wt, ctr, w, b, offs, out):
         b_sb = held.tile([P, MB], F32)
         nc.sync.dma_start(b_sb[:], b.rearrange("(p q) o -> p (q o)", q=MB))
 
+        zeros = held.tile([P, CHUNK], BF16)
+        nc.vector.memset(zeros[:], 0.0)
+        idle = psum.tile([P, CHUNK], F32, name="bank")
+        for i in range(WARM_UP):
+            nc.tensor.matmul(idle[:], zeros[:, :P], zeros[:], start=True, stop=True)
+
         tables = []
         for r in range(RB):
             table = held.tile([P, S], F32, name=f"table{r}")
@@ -49,29 +57,39 @@ def tile_lookup_pjedge_relu_kernel(tc, z, wt, ctr, w, b, offs, out):
                     nc.scalar.copy(table[:, cols], bank[:])
             tables.append(table)
 
-        xs = []
-        for r in range(RB):
+        def summed_parts(r, x, cols):
             diffs = []
             for d in range(D):
-                diff = work.tile([P, V], F32, name=f"diff{d}")
-                entries = offsets[:, d * V // 16:(d + 1) * V // 16]
-                nc.vector.tensor_tensor(diff[:], tables[r][:].indirect(entries), ctr_sb[:, r, :], SUBTRACT)
+                diff = work.tile([P, cols.stop - cols.start], F32, name=f"diff{r}{d}")
+                entries = offsets[:, (d * V + cols.start) // 16:(d * V + cols.stop) // 16]
+                nc.vector.tensor_tensor(diff[:], tables[r][:].indirect(entries), ctr_sb[:, r, cols], SUBTRACT)
                 diffs.append(diff)
-            first = work.tile([P, V], F32, name="first")
+            first = work.tile([P, cols.stop - cols.start], F32, name=f"first{r}")
             nc.scalar.activation(first[:], diffs[0][:], RELU)
-            x = held.tile([P, V], BF16, name=f"x{r}")
-            nc.vector.scalar_tensor_tensor(x[:], diffs[1][:], 0.0, first[:], MAX, ADD)
-            xs.append(x)
+            nc.vector.scalar_tensor_tensor(x[:, cols], diffs[1][:], 0.0, first[:], MAX, ADD)
 
+        halves = [slice(h * HALF, (h + 1) * HALF) for h in range(2)]
+        xs = [held.tile([P, V], BF16, name=f"x{r}") for r in range(RB)]
+        sums = {(h, q): psum.tile([P, HALF], F32, name="bank") for h in range(2) for q in range(MB)}
         out_sb = held.tile([P, MB, V], F32)
         out_view = out.rearrange("(p q) j -> p q j", q=MB)
-        sums = [psum.tile([P, V], F32, name="bank") for q in range(MB)]
-        for r in range(RB):
+
+        def layer(r, h):
             for q in range(MB):
-                nc.tensor.matmul(sums[q][:], w_sb[:, r, q::MB], xs[r][:], start=r == 0, stop=r == RB - 1)
-        for q in range(MB):
-            if q % 2 == 0:
-                nc.scalar.activation(out_sb[:, q, :], sums[q][:], RELU, bias=b_sb[:, q:q + 1])
-            else:
-                nc.vector.tensor_scalar(out_sb[:, q, :], sums[q][:], b_sb[:, q:q + 1], 0.0, ADD, MAX)
-            nc.sync.dma_start(out_view[:, q, :], out_sb[:, q, :])
+                nc.tensor.matmul(sums[h, q][:], w_sb[:, r, q::MB], xs[r][:, halves[h]],
+                                 start=r == 0, stop=r == RB - 1)
+
+        summed_parts(0, xs[0], slice(0, V))
+        layer(0, 0)
+        layer(0, 1)
+        summed_parts(1, xs[1], halves[0])
+        summed_parts(1, xs[1], halves[1])
+        for h, cols in enumerate(halves):
+            layer(1, h)
+            for q in range(MB):
+                if h == 0 or q % 2 == 0:
+                    nc.scalar.activation(out_sb[:, q, cols], sums[h, q][:], RELU, bias=b_sb[:, q:q + 1])
+                else:
+                    nc.vector.tensor_scalar(out_sb[:, q, cols], sums[h, q][:], b_sb[:, q:q + 1], 0.0, ADD, MAX)
+                if q % 2 == 1:
+                    nc.sync.dma_start(out_view[:, q - 1:q + 1, cols], out_sb[:, q - 1:q + 1, cols])

@@ -8,7 +8,7 @@ P = 128
 H, S, R, D, V, M = 256, 2048, 256, 2, 512, 512
 KB, RB, MB = H // P, R // P, M // P
 HALF = V // 2
-WARM_UP = 5
+WARM_UP = 8
 CHUNK = 512
 FLOPS = 2 * H * R * S + 2 * R * M * V + 3 * R * D * V
 
@@ -24,8 +24,9 @@ def tile_lookup_pjedge_relu_kernel(tc, z, wt, ctr, w, b, offs, out):
         nc.sync.dma_start(wt_sb[:], wt.rearrange("(k p) r -> p k r", p=P))
         z_sb = held.tile([P, KB, S], BF16)
         z_view = z.rearrange("(k p) s -> p k s", p=P)
-        for c in range(S // CHUNK):
-            cols = slice(c * CHUNK, (c + 1) * CHUNK)
+        chunks = [slice(c, c + CHUNK) for c in range(0, S - CHUNK, CHUNK)]
+        chunks += [slice(S - 2 * HALF, S - HALF), slice(S - HALF, S)]
+        for cols in chunks:
             nc.sync.dma_start(z_sb[:, :, cols], z_view[:, :, cols])
         offsets = held.tile([P, D * V // 16], U16)
         nc.sync.dma_start(offsets[:], offs)
@@ -36,26 +37,24 @@ def tile_lookup_pjedge_relu_kernel(tc, z, wt, ctr, w, b, offs, out):
         b_sb = held.tile([P, MB], F32)
         nc.sync.dma_start(b_sb[:], b.rearrange("(p q) o -> p (q o)", q=MB))
 
-        zeros = held.tile([P, CHUNK], BF16)
+        zeros = held.tile([P, HALF], BF16)
         nc.vector.memset(zeros[:], 0.0)
         idle = psum.tile([P, CHUNK], F32, name="bank")
         for i in range(WARM_UP):
-            nc.tensor.matmul(idle[:], zeros[:, :P], zeros[:], start=True, stop=True)
+            nc.tensor.matmul(idle[:, :HALF], zeros[:, :P], zeros[:], start=True, stop=True)
 
-        tables = []
-        for r in range(RB):
-            table = held.tile([P, S], F32, name=f"table{r}")
-            for c in range(S // CHUNK):
-                cols = slice(c * CHUNK, (c + 1) * CHUNK)
-                bank = psum.tile([P, CHUNK], F32, name="bank")
+        tables = [held.tile([P, S], F32, name=f"table{r}") for r in range(RB)]
+
+        def project(r):
+            for c, cols in enumerate(chunks):
+                bank = psum.tile([P, cols.stop - cols.start], F32, name="bank")
                 for k in range(KB):
                     nc.tensor.matmul(bank[:], wt_sb[:, k, r * P:(r + 1) * P], z_sb[:, k, cols],
                                      start=k == 0, stop=k == KB - 1)
                 if r == 0 and c % 2 == 1:
-                    nc.vector.tensor_copy(table[:, cols], bank[:])
+                    nc.vector.tensor_copy(tables[r][:, cols], bank[:])
                 else:
-                    nc.scalar.copy(table[:, cols], bank[:])
-            tables.append(table)
+                    nc.scalar.copy(tables[r][:, cols], bank[:])
 
         def summed_parts(r, x, cols):
             diffs = []
@@ -79,7 +78,9 @@ def tile_lookup_pjedge_relu_kernel(tc, z, wt, ctr, w, b, offs, out):
                 nc.tensor.matmul(sums[h, q][:], w_sb[:, r, q::MB], xs[r][:, halves[h]],
                                  start=r == 0, stop=r == RB - 1)
 
+        project(0)
         summed_parts(0, xs[0], slice(0, V))
+        project(1)
         layer(0, 0)
         layer(0, 1)
         summed_parts(1, xs[1], halves[0])

import concourse.mybir as mybir

BF16, F32, U16 = mybir.dt.bfloat16, mybir.dt.float32, mybir.dt.uint16
RELU = mybir.ActivationFunctionType.Relu
ADD, MAX, SUBTRACT = mybir.AluOpType.add, mybir.AluOpType.max, mybir.AluOpType.subtract

P = 128
H, S, R, D, V, M = 256, 2048, 256, 2, 512, 512
KB, RB, MB = H // P, R // P, M // P
HALF = V // 2
WARM_UP = 8
CHUNK = 512
FLOPS = 2 * H * R * S + 2 * R * M * V + 3 * R * D * V


def tile_lookup_pjedge_relu_kernel(tc, z, wt, ctr, w, b, offs, out):
    nc = tc.nc
    with (
        tc.tile_pool(name="held", bufs=1) as held,
        tc.tile_pool(name="work", bufs=2) as work,
        tc.psum_pool(name="psum", bufs=8) as psum,
    ):
        wt_sb = held.tile([P, KB, R], BF16)
        nc.sync.dma_start(wt_sb[:], wt.rearrange("(k p) r -> p k r", p=P))
        z_sb = held.tile([P, KB, S], BF16)
        z_view = z.rearrange("(k p) s -> p k s", p=P)
        chunks = [slice(c, c + CHUNK) for c in range(0, S - CHUNK, CHUNK)]
        chunks += [slice(S - 2 * HALF, S - HALF), slice(S - HALF, S)]
        for cols in chunks:
            nc.sync.dma_start(z_sb[:, :, cols], z_view[:, :, cols])
        offsets = held.tile([P, D * V // 16], U16)
        nc.sync.dma_start(offsets[:], offs)
        ctr_sb = held.tile([P, RB, V], F32)
        nc.sync.dma_start(ctr_sb[:], ctr.rearrange("(r p) j -> p r j", p=P))
        w_sb = held.tile([P, RB, M], BF16)
        nc.sync.dma_start(w_sb[:], w.rearrange("(r p) m -> p r m", p=P))
        b_sb = held.tile([P, MB], F32)
        nc.sync.dma_start(b_sb[:], b.rearrange("(p q) o -> p (q o)", q=MB))

        zeros = held.tile([P, HALF], BF16)
        nc.vector.memset(zeros[:], 0.0)
        idle = psum.tile([P, CHUNK], F32, name="bank")
        for i in range(WARM_UP):
            nc.tensor.matmul(idle[:, :HALF], zeros[:, :P], zeros[:], start=True, stop=True)

        tables = [held.tile([P, S], F32, name=f"table{r}") for r in range(RB)]

        def project(r):
            for c, cols in enumerate(chunks):
                bank = psum.tile([P, cols.stop - cols.start], F32, name="bank")
                for k in range(KB):
                    nc.tensor.matmul(bank[:], wt_sb[:, k, r * P:(r + 1) * P], z_sb[:, k, cols],
                                     start=k == 0, stop=k == KB - 1)
                if r == 0 and c % 2 == 1:
                    nc.vector.tensor_copy(tables[r][:, cols], bank[:])
                else:
                    nc.scalar.copy(tables[r][:, cols], bank[:])

        def summed_parts(r, x, cols):
            diffs = []
            for d in range(D):
                diff = work.tile([P, cols.stop - cols.start], F32, name=f"diff{r}{d}")
                entries = offsets[:, (d * V + cols.start) // 16:(d * V + cols.stop) // 16]
                nc.vector.tensor_tensor(diff[:], tables[r][:].indirect(entries), ctr_sb[:, r, cols], SUBTRACT)
                diffs.append(diff)
            first = work.tile([P, cols.stop - cols.start], F32, name=f"first{r}")
            nc.scalar.activation(first[:], diffs[0][:], RELU)
            nc.vector.scalar_tensor_tensor(x[:, cols], diffs[1][:], 0.0, first[:], MAX, ADD)

        halves = [slice(h * HALF, (h + 1) * HALF) for h in range(2)]
        xs = [held.tile([P, V], BF16, name=f"x{r}") for r in range(RB)]
        sums = {(h, q): psum.tile([P, HALF], F32, name="bank") for h in range(2) for q in range(MB)}
        out_sb = held.tile([P, MB, V], F32)
        out_view = out.rearrange("(p q) j -> p q j", q=MB)

        def layer(r, h):
            for q in range(MB):
                nc.tensor.matmul(sums[h, q][:], w_sb[:, r, q::MB], xs[r][:, halves[h]],
                                 start=r == 0, stop=r == RB - 1)

        project(0)
        summed_parts(0, xs[0], slice(0, V))
        project(1)
        layer(0, 0)
        layer(0, 1)
        summed_parts(1, xs[1], halves[0])
        summed_parts(1, xs[1], halves[1])
        for h, cols in enumerate(halves):
            layer(1, h)
            for q in range(MB):
                if h == 0 or q % 2 == 0:
                    nc.scalar.activation(out_sb[:, q, cols], sums[h, q][:], RELU, bias=b_sb[:, q:q + 1])
                else:
                    nc.vector.tensor_scalar(out_sb[:, q, cols], sums[h, q][:], b_sb[:, q:q + 1], 0.0, ADD, MAX)
                if q % 2 == 1:
                    nc.sync.dma_start(out_view[:, q - 1:q + 1, cols], out_sb[:, q - 1:q + 1, cols])
